import numpy as np
CORES = [0,1,2,3,4,5,6,7]
N = 8
def setup_inputs(rng):
    return {"x": rng.standard_normal((N, 128, 2048), dtype=np.float32)}
def reference(x):
    b = 2048 // N
    blocks = x.reshape(N, 128, N, b)
    return {"y": np.ascontiguousarray(blocks.transpose(2, 1, 0, 3)).reshape(N, 128, 2048)}

from concourse.bass import DstId, RemoteDMATransfer

N = 8
B = 2048 // N
ENG = 2

SCRATCH = {
    "send": ("sbuf", [128, (N - 1) * B], "float32"),
    "land": ("sbuf", [128, (N - 1) * B], "float32"),
}
SEMAPHORES = ["loaded", "sent", "arr_lo", "arr_hi", "stored"]


def rank_program(g, core, T, topo):
    r = T.rank_of(core)
    if r is None:
        return
    lo = r * B
    hi = (N - 1 - r) * B
    own = slice(lo, lo + B)

    loads = 0
    if lo:
        g.sync.dma_start(T.send[:, :lo], T.x[:, :lo]).then_inc(T.sem.loaded, 16)
        loads += 16
    if hi:
        g.scalar.dma_start(T.send[:, lo:], T.x[:, lo + B:]).then_inc(T.sem.loaded, 16)
        loads += 16

    q_own = g.sync if lo <= hi else g.scalar
    q_own.dma_start(T.y[:, own], T.x[:, own]).then_inc(T.sem.stored, 16)
    stores = 16

    g.wait_ge(T.sem.loaded, loads)
    transfers = []
    for d in range(N):
        if d == r:
            continue
        k = len(transfers)
        slot = r if r < d else r - 1
        rid, pid, _se = topo.addr(T.cores[d])
        transfers.append(RemoteDMATransfer(
            dst_ids=[DstId(rid=rid, pnc=pid)],
            dma_engine_mask=((1 << ENG) - 1) << (ENG * k),
            remote_sem=T.sem.arr_lo if r < d else T.sem.arr_hi,
            src=T.send[:, k * B:(k + 1) * B],
            dst=T.land[:, slot * B:(slot + 1) * B],
        ))
    g.remote_dma_fused(transfers, local_sem=T.sem.sent)

    if lo:
        g.sync.wait_ge(T.sem.arr_lo, ENG * r)
        g.sync.dma_start(T.y[:, :lo], T.land[:, :lo]).then_inc(T.sem.stored, 16)
        stores += 16
    if hi:
        g.scalar.wait_ge(T.sem.arr_hi, ENG * (N - 1 - r))
        g.scalar.dma_start(T.y[:, lo + B:], T.land[:, lo:]).then_inc(T.sem.stored, 16)
        stores += 16

    g.wait_ge(T.sem.sent, ENG * (N - 1))
    g.wait_ge(T.sem.stored, stores)
